import numpy as np
import ml_dtypes


def mxq(x, axis, fmt="e4m3"):
    dtype, down = {"e4m3": (ml_dtypes.float8_e4m3fn, 7), "e5m2": (ml_dtypes.float8_e5m2, 14)}[fmt]
    v = np.moveaxis(np.asarray(x, np.float32).astype(ml_dtypes.bfloat16).astype(np.float64), axis, -1)
    blocks = v.reshape(v.shape[:-1] + (-1, 32))
    amax = np.abs(blocks).max(-1, keepdims=True)
    byte = np.maximum(np.where(amax > 0, np.frexp(amax)[1] - 1 + 127, 0) - down, 1)
    scale = np.exp2(byte - 127.0)
    codes = (blocks / scale).astype(np.float32).astype(dtype).astype(np.float64)
    return np.moveaxis((codes * scale).reshape(v.shape), -1, axis)


WIDE = False


def mx_kscale(k):
    if not WIDE:
        return np.ones(k)
    levels = np.array([10, -10, 5, -5, 0])
    if k % 512:
        return np.exp2(np.random.permutation(np.resize(levels, k // 32))).repeat(32)
    a = np.empty((k // 512, 16))
    for p in range(k // 512):
        a[p, :8] = np.random.permutation(np.resize(levels, 8))
        for g in range(8):
            far = levels[np.abs(levels - a[p, g]) >= 10]
            a[p, g + 8] = far[np.random.randint(len(far))]
    return np.exp2(a.ravel()).repeat(32)


def f64(x):
    return np.asarray(x).astype(np.float64)


def striped(idx):
    return np.tile(np.asarray(idx).reshape(-1, 16).T, (8, 1)).astype(np.uint16)


def unstriped(offs):
    return offs[:16].T.reshape(-1).astype(np.int64)


E2M1 = np.array([0.0, 0.5, 1.0, 1.5, 2.0, 3.0, 4.0, 6.0, -0.0, -0.5, -1.0, -1.5, -2.0, -3.0, -4.0, -6.0])


def pack_weight(w, fmt):
    k, n = w.shape
    w = f64(np.asarray(w, np.float32).astype(ml_dtypes.bfloat16)).reshape(k // 32, 32, n)
    amax = np.abs(w).max(1)
    if fmt == "e4m3":
        byte = np.frexp(amax)[1] - 1 + 127 - 7
    else:
        mant, ex = np.frexp(amax / 6.0)
        byte = np.where(mant > 0.5, ex, ex - 1) + 127
    byte = np.clip(np.where(amax > 0, byte, 1), 1, 254)
    scaled = (w * np.exp2(127.0 - byte)[:, None, :]).reshape(k, n).astype(np.float32)
    by_word = np.ascontiguousarray(scaled.reshape(k // 512, 128, 4, n).transpose(0, 1, 3, 2))
    if fmt == "e4m3":
        words = by_word.astype(ml_dtypes.float8_e4m3fn).view(np.uint8)
    else:
        c = by_word.astype(ml_dtypes.float4_e2m1fn).view(np.uint8) & 0xF
        words = (c[..., 0::2] | (c[..., 1::2] << 4)).reshape(k // 512, 128, 2 * n)
    return np.ascontiguousarray(words), np.ascontiguousarray(byte.astype(np.uint8).reshape(k // 512, 16, n))


def unpack_weight(words, scales, fmt):
    g, _, n = scales.shape
    words = np.ascontiguousarray(words).reshape(g, 128, n, -1)
    if fmt == "e4m3":
        vals = words.view(ml_dtypes.float8_e4m3fn).astype(np.float64)
    else:
        nib = np.empty((g, 128, n, 4), np.uint8)
        nib[..., 0::2] = words & 0xF
        nib[..., 1::2] = words >> 4
        vals = E2M1[nib]
    vals = vals * np.repeat(np.exp2(scales.astype(np.float64) - 127.0), 8, axis=1)[..., None]
    return vals.transpose(0, 1, 3, 2).reshape(g * 512, n)


def softplus(v):
    return np.log(1.0 + np.exp(v))


def sigmoid(v):
    return 1.0 / (1.0 + np.exp(-v))


def bf(x):
    return np.asarray(x, np.float32).astype(ml_dtypes.bfloat16)


def planes(Y):
    r, m = Y.shape
    b = f64(bf(Y)).reshape(r // 32, 32, m)
    amax = np.abs(b).max(1)
    byte = np.clip(np.where(amax > 0, np.frexp(amax)[1] - 1 + 127 - 7, 1), 1, 254)
    codes = (b * np.exp2(127.0 - byte)[:, None, :]).reshape(r, m).astype(np.float32).astype(ml_dtypes.float8_e4m3fn).view(np.uint8)
    words = codes.reshape(r // 512, 128, 4, m).transpose(0, 1, 3, 2)
    return np.ascontiguousarray(words), np.ascontiguousarray(byte.astype(np.uint8).reshape(r // 512, 16, m))


K, R, F, T, J, M = 512, 512, 512, 2048, 512, 256


def setup_inputs():
    n = np.random.standard_normal
    idx = np.random.permutation(T)[:J]
    idx2 = np.random.permutation(J)[:M]
    idx3 = np.random.permutation(J)[:M]
    fk = mx_kscale(K)
    fr = mx_kscale(R)
    tabp = pack_weight(n((K, T)) / fk[:, None], "e2m1")
    dtabp = pack_weight(n((K, T)) / fk[:, None], "e2m1")
    return {
        "tab_words": tabp[0],
        "tab_scales": tabp[1],
        "dtab_words": dtabp[0],
        "dtab_scales": dtabp[1],
        "w1": (n((K, R)) * 1 / np.sqrt(K) * fk[:, None]).astype(np.float32),
        "bias": (np.random.uniform(-0.5, 0.5, (R, 1))).astype(np.float32),
        "reserve": (np.random.uniform(0.3, 1.0, (R, 1))).astype(np.float32),
        "rs": (np.random.uniform(0.5, 2.0, (R, 1)) * fr[:, None]).astype(np.float32),
        "wor": (n((R, F)) * 1 / np.sqrt(R) / fr[:, None]).astype(np.float32),
        "res": (n((F, M)) * 0.5).astype(np.float32),
        "offs": striped(idx),
        "offs2": striped(idx2),
        "offs3": striped(idx3),
    }


def reference(tab_words, tab_scales, dtab_words, dtab_scales, w1, bias, reserve, rs, wor, res, offs, offs2, offs3):
    idx = unstriped(offs)
    idx2 = unstriped(offs2)
    idx3 = unstriped(offs3)
    tabu = unpack_weight(tab_words, tab_scales, "e2m1")
    dtabu = unpack_weight(dtab_words, dtab_scales, "e2m1")
    w1q = mxq(f64(w1), 0, "e4m3")
    tabidxg = tabu[:, idx]
    a = w1q.T @ tabidxg
    dtabidxg = dtabu[:, idx]
    ta = w1q.T @ dtabidxg
    h1 = softplus(a + f64(bias))
    s = h1[:, idx2] * h1[:, idx3]
    th1 = ta * sigmoid(a + f64(bias))
    ts = th1[:, idx2] * h1[:, idx3] + th1[:, idx3] * h1[:, idx2]
    tu1 = (ts - (ts + th1[:, idx2]) * s / (s + h1[:, idx2] + f64(reserve))) / (s + h1[:, idx2] + f64(reserve))
    fo1 = tu1 * f64(rs)
    worq = mxq(f64(wor), 0, "e4m3")
    fo1q = mxq(fo1, 0, "e4m3")
    yo = worq.T @ fo1q
    y = yo + f64(res)
    words, scales = planes(y)
    return y, words, scales

@@ -1,0 +1,209 @@
+from contextlib import ExitStack
+
+import concourse.mybir as mybir
+
+K, R, F, T, J, M = 512, 512, 512, 2048, 512, 256
+FLOPS = 2 * K * R * J * 2 + 2 * R * F * M
+
+F32 = mybir.dt.float32
+BF16 = mybir.dt.bfloat16
+I32 = mybir.dt.int32
+U32 = mybir.dt.uint32
+U16 = mybir.dt.uint16
+U8 = mybir.dt.uint8
+FP8X4 = mybir.dt.float8_e4m3fn_x4
+FP4X4 = mybir.dt.float4_e2m1fn_x4
+ALU = mybir.AluOpType
+ACT = mybir.ActivationFunctionType
+
+P = 128
+PACK = 4
+HALF = M // 2
+FLOOR = 2.0**-60
+
+
+def tile_attend_tcpairshare_o_pl_kernel(tc, tab_words, tab_scales, dtab_words, dtab_scales, w1, bias, reserve, rs, wor, res, offs, offs2, offs3, out_0, out_1, out_2):
+    nc = tc.nc
+    with ExitStack() as ctx:
+        lists = ctx.enter_context(tc.tile_pool(name="lists", bufs=1))
+        keep = ctx.enter_context(tc.tile_pool(name="keep", bufs=1))
+        psum = ctx.enter_context(tc.psum_pool(name="psum", bufs=1))
+
+        def sb(name, shape, dtype):
+            return keep.tile(shape, dtype, name=name, align_bytes=64)
+
+        def per_tile(name, width, dtype=F32):
+            return [sb("%s%d" % (name, t), [P, width], dtype) for t in range(PACK)]
+
+        slots = lists.tile([P, J // 16], U16, name="slots")
+        first = lists.tile([P, M // 16], U16, name="first")
+        second = lists.tile([P, M // 16], U16, name="second")
+
+        tab_w = sb("tab_w", [P, T], U16)
+        tab_s = sb("tab_s", [P, T], U8)
+        dtab_w = sb("dtab_w", [P, T], U16)
+        dtab_s = sb("dtab_s", [P, T], U8)
+        w1_raw = [sb("w1_raw%d" % h, [P, PACK, R // 2], F32) for h in range(2)]
+        wor_raw = sb("wor_raw", [P, PACK, F], F32)
+        res_sb = sb("res_sb", [P, PACK, M], F32)
+        bias_sb = sb("bias_sb", [P, PACK], F32)
+        reserve_sb = sb("reserve_sb", [P, PACK], F32)
+        rs_sb = sb("rs_sb", [P, PACK], F32)
+
+        def load_scales(tile, scales):
+            for q in range(4):
+                nc.sync.dma_start(out=tile[32 * q : 32 * q + 4, :].bitcast(I32), in_=scales[0, 4 * q : 4 * q + 4, :].bitcast(I32))
+
+        nc.vector.memset(tab_s[:].bitcast(I32), 0)
+        nc.vector.memset(dtab_s[:].bitcast(I32), 0)
+        warm = sb("warm", [P, 1], F32)
+        warm_out = sb("warm_out", [P, 1], F32)
+        nc.vector.memset(warm[:], 0.0)
+        nc.scalar.activation(warm_out[:], warm[:], ACT.Sigmoid)
+
+        def load_column(tile, column):
+            nc.sync.dma_start(out=tile[:], in_=column.rearrange("(p t) o -> p (t o)", t=PACK))
+
+        nc.sync.dma_start(slots[:], offs)
+        nc.sync.dma_start(out=tab_w[:].bitcast(I32), in_=tab_words[0].bitcast(I32))
+        load_scales(tab_s, tab_scales)
+        w1_rows = w1.rearrange("(p j) c -> p j c", j=PACK)
+        for h in range(2):
+            nc.sync.dma_start(out=w1_raw[h][:], in_=w1_rows[:, :, h * (R // 2) : (h + 1) * (R // 2)])
+        load_column(bias_sb, bias)
+        nc.sync.dma_start(out=dtab_w[:].bitcast(I32), in_=dtab_words[0].bitcast(I32))
+        load_scales(dtab_s, dtab_scales)
+        nc.sync.dma_start(out=wor_raw[:], in_=wor.rearrange("(p j) c -> p j c", j=PACK))
+        nc.sync.dma_start(first[:], offs2)
+        nc.sync.dma_start(second[:], offs3)
+        load_column(reserve_sb, reserve)
+        load_column(rs_sb, rs)
+        nc.sync.dma_start(out=res_sb[:], in_=res.rearrange("(p t) m -> p t m", t=PACK))
+
+        neg_bias = sb("neg_bias", [P, PACK], F32)
+        half_c = sb("half_c", [P, PACK], F32)
+        c_rs = sb("c_rs", [P, PACK], F32)
+        neg_quarter = sb("neg_quarter", [P, PACK], F32)
+        nc.scalar.activation(neg_bias[:], bias_sb[:], ACT.Copy, scale=-1.0)
+
+        tab_gw = sb("tab_gw", [P, J], U16)
+        tab_gs = sb("tab_gs", [P, J], U8)
+        dtab_gw = sb("dtab_gw", [P, J], U16)
+        dtab_gs = sb("dtab_gs", [P, J], U8)
+        nc.vector.tensor_copy(tab_gw[:], tab_w[:].indirect(slots[:]))
+        nc.vector.tensor_copy(tab_gs[:], tab_s[:].indirect(slots[:]))
+
+        w1_bf = sb("w1_bf", [P, PACK, P, PACK], BF16)
+        w1_codes = sb("w1_codes", [P, R], U32)
+        w1_scales = sb("w1_scales", [P, R], U8)
+        for h, copy in enumerate((nc.scalar.copy, nc.vector.tensor_copy)):
+            copy(
+                w1_bf[:, :, h * (P // 2) : (h + 1) * (P // 2), :].rearrange("p t m j -> p m j t"),
+                w1_raw[h][:].rearrange("p j (m t) -> p m j t", t=PACK),
+            )
+        a_ps = [psum.tile([P, J], F32, name="a_ps%d" % t) for t in range(PACK)]
+        ta_ps = [psum.tile([P, J], F32, name="ta_ps%d" % t) for t in range(PACK)]
+
+        def first_layer(bank, t, words, scales):
+            cols = slice(t * P, (t + 1) * P)
+            nc.tensor.matmul_mx(out=bank[:], lhsT=w1_codes[:, cols].bitcast(FP8X4), lhsT_scale=w1_scales[:, cols], rhs=words[:].bitcast(FP4X4), rhs_scale=scales[:], start=True, stop=True)
+
+        for t in range(PACK):
+            cols = slice(t * P, (t + 1) * P)
+            nc.vector.quantize_mx(out=w1_codes[:, cols].bitcast(FP8X4), scales=w1_scales[:, cols], in_=w1_bf[:, t, :, :].rearrange("p m j -> p (m j)"))
+            first_layer(a_ps[t], t, tab_gw, tab_gs)
+
+        nc.vector.tensor_copy(dtab_gw[:], dtab_w[:].indirect(slots[:]))
+        nc.vector.tensor_copy(dtab_gs[:], dtab_s[:].indirect(slots[:]))
+        for t in range(PACK):
+            first_layer(ta_ps[t], t, dtab_gw, dtab_gs)
+
+        sig = per_tile("sig", J)
+        sig_neg = per_tile("sig_neg", J)
+        x = per_tile("x", J)
+        log_neg = per_tile("log_neg", J)
+        h1 = per_tile("h1", J)
+        th1 = per_tile("th1", J)
+        for t in range(PACK):
+            nc.scalar.activation(sig[t][:], a_ps[t][:], ACT.Sigmoid, bias=bias_sb[:, t : t + 1])
+            nc.scalar.activation(sig_neg[t][:], a_ps[t][:], ACT.Sigmoid, bias=neg_bias[:, t : t + 1], scale=-1.0)
+        for t in range(PACK):
+            nc.vector.tensor_tensor(th1[t][:], ta_ps[t][:], sig[t][:], ALU.mult)
+        nc.vector.tensor_scalar(x[0][:], a_ps[0][:], bias_sb[:, 0:1], None, ALU.add)
+
+        wor_bf = sb("wor_bf", [P, PACK, P, PACK], BF16)
+        wor_codes = sb("wor_codes", [P, F], U32)
+        wor_scales = sb("wor_scales", [P, F], U8)
+        nc.vector.tensor_copy(wor_bf[:].rearrange("p t m j -> p m j t"), wor_raw[:].rearrange("p j (m t) -> p m j t", t=PACK))
+        nc.vector.quantize_mx(out=wor_codes[:].bitcast(FP8X4), scales=wor_scales[:], in_=wor_bf[:].rearrange("p t m j -> p (t m j)"))
+
+        nc.vector.tensor_scalar(half_c[:], reserve_sb[:], 0.5, None, ALU.mult)
+        nc.vector.tensor_tensor(c_rs[:], reserve_sb[:], rs_sb[:], ALU.mult)
+        nc.vector.scalar_tensor_tensor(neg_quarter[:], c_rs[:], -0.25, reserve_sb[:], ALU.mult, ALU.mult)
+        ga = per_tile("ga", M)
+        gb = per_tile("gb", M)
+        dpart = per_tile("dpart", M)
+        sq = per_tile("sq", M)
+        u = per_tile("u", M)
+        t1 = per_tile("t1", M)
+        t2 = per_tile("t2", M)
+        num = per_tile("num", M)
+        d_abs = sb("d_abs", [P, PACK * M], F32)
+        d_log = sb("d_log", [P, PACK * M], F32)
+        inv_sq = sb("inv_sq", [P, PACK * M], F32)
+        fo = sb("fo", [P, PACK, M], BF16)
+
+        for t in range(PACK):
+            nc.scalar.activation(log_neg[t][:], sig_neg[t][:], ACT.Ln, bias=FLOOR)
+            if t > 0:
+                nc.scalar.activation(x[t][:], a_ps[t][:], ACT.Identity, bias=bias_sb[:, t : t + 1])
+        for t in range(PACK):
+            nc.vector.scalar_tensor_tensor(h1[t][:], log_neg[t][:], -1.0, x[t][:], ALU.mult, ALU.max)
+            nc.vector.tensor_copy(ga[t][:], h1[t][:].indirect(first[:]))
+            nc.vector.tensor_copy(gb[t][:], h1[t][:].indirect(second[:]))
+            nc.vector.scalar_tensor_tensor(dpart[t][:], gb[t][:], 1.0, ga[t][:], ALU.add, ALU.mult)
+            nc.scalar.activation(d_abs[:, t * M : (t + 1) * M], dpart[t][:], ACT.Abs, bias=reserve_sb[:, t : t + 1])
+        nc.scalar.activation(d_log[:], d_abs[:], ACT.Ln)
+        nc.scalar.activation(inv_sq[:], d_log[:], ACT.Exp, scale=-2.0)
+        for t in range(PACK):
+            nc.scalar.activation(sq[t][:], ga[t][:], ACT.Square, bias=half_c[:, t : t + 1])
+            nc.scalar.activation(u[t][:], sq[t][:], ACT.Identity, bias=neg_quarter[:, t : t + 1], scale=rs_sb[:, t : t + 1])
+        for t in range(PACK):
+            nc.vector.tensor_tensor(t2[t][:], th1[t][:].indirect(first[:]), gb[t][:], ALU.mult)
+            nc.vector.tensor_tensor(t1[t][:], th1[t][:].indirect(second[:]), u[t][:], ALU.mult)
+            nc.vector.scalar_tensor_tensor(num[t][:], t2[t][:], c_rs[:, t : t + 1], t1[t][:], ALU.mult, ALU.add)
+            nc.vector.tensor_tensor(fo[:, t, :], num[t][:], inv_sq[:, t * M : (t + 1) * M], ALU.mult)
+
+        y_codes = sb("y_codes", [P, M], U32)
+        y_scales = sb("y_scales", [P, M], U8)
+        out_rows = out_0.rearrange("(p t) m -> p t m", t=PACK)
+        out_words = out_1[0].rearrange("p m t -> p (m t)").bitcast(I32)
+
+        def interleave(copy, dst, src):
+            copy(dst.rearrange("p (c i) t -> p c t i", i=4), src.rearrange("p t (c i) -> p c t i", i=4))
+
+        fo_il = [sb("fo_il%d" % h, [P, HALF, PACK], BF16) for h in range(2)]
+        fo_codes = [sb("fo_codes%d" % h, [P, HALF], U32) for h in range(2)]
+        fo_scales = [sb("fo_scales%d" % h, [P, HALF], U8) for h in range(2)]
+        y = [sb("y%d" % h, [P, PACK, HALF], F32) for h in range(2)]
+        y_il = [sb("y_il%d" % h, [P, HALF, PACK], BF16) for h in range(2)]
+        halves = [slice(h * HALF, (h + 1) * HALF) for h in range(2)]
+        interleave(nc.vector.tensor_copy, fo_il[0][:], fo[:, :, halves[0]])
+        interleave(nc.scalar.copy, fo_il[1][:], fo[:, :, halves[1]])
+        yo_ps = []
+        for h in range(2):
+            nc.vector.quantize_mx(out=fo_codes[h][:].bitcast(FP8X4), scales=fo_scales[h][:], in_=fo_il[h][:].rearrange("p m t -> p (m t)"))
+            bank = psum.tile([P, J], F32, name="a_ps%d" % h)
+            yo_ps.append(bank)
+            for t in range(PACK):
+                cols = slice(t * P, (t + 1) * P)
+                nc.tensor.matmul_mx(out=bank[:, t * HALF : (t + 1) * HALF], lhsT=wor_codes[:, cols].bitcast(FP8X4), lhsT_scale=wor_scales[:, cols], rhs=fo_codes[h][:].bitcast(FP8X4), rhs_scale=fo_scales[h][:], start=True, stop=True)
+        for h in range(2):
+            nc.vector.tensor_tensor(y[h][:], yo_ps[h][:].rearrange("p (t m) -> p t m", t=PACK), res_sb[:, :, halves[h]], ALU.add)
+            nc.sync.dma_start(out=out_rows[:, :, halves[h]], in_=y[h][:])
+            interleave(nc.scalar.copy, y_il[h][:], y[h][:])
+        for h in range(2):
+            nc.vector.quantize_mx(out=y_codes[:, halves[h]].bitcast(FP8X4), scales=y_scales[:, halves[h]], in_=y_il[h][:].rearrange("p m t -> p (m t)"))
+        nc.sync.dma_start(out=out_words, in_=y_codes[:].bitcast(I32))
+        for q in range(4):
+            nc.sync.dma_start(out=out_2[0, 4 * q : 4 * q + 4, :].bitcast(I32), in_=y_scales[32 * q : 32 * q + 4, :].bitcast(I32))

@@ -29,8 +29,8 @@ def tile_attend_tcpairshare_o_pl_kernel(tc, tab_words, tab_scales, dtab_words, d
         keep = ctx.enter_context(tc.tile_pool(name="keep", bufs=1))
         psum = ctx.enter_context(tc.psum_pool(name="psum", bufs=1))
 
-        def sb(name, shape, dtype):
-            return keep.tile(shape, dtype, name=name, align_bytes=64)
+        def sb(name, shape, dtype, tag=None):
+            return keep.tile(shape, dtype, name=name, tag=tag or name, align_bytes=64)
 
         def per_tile(name, width, dtype=F32):
             return [sb("%s%d" % (name, t), [P, width], dtype) for t in range(PACK)]
@@ -73,11 +73,11 @@ def tile_attend_tcpairshare_o_pl_kernel(tc, tab_words, tab_scales, dtab_words, d
         load_column(bias_sb, bias)
         nc.sync.dma_start(out=dtab_w[:].bitcast(I32), in_=dtab_words[0].bitcast(I32))
         load_scales(dtab_s, dtab_scales)
-        nc.sync.dma_start(out=wor_raw[:], in_=wor.rearrange("(p j) c -> p j c", j=PACK))
         nc.sync.dma_start(first[:], offs2)
         nc.sync.dma_start(second[:], offs3)
         load_column(reserve_sb, reserve)
         load_column(rs_sb, rs)
+        nc.sync.dma_start(out=wor_raw[:], in_=wor.rearrange("(p j) c -> p j c", j=PACK))
         nc.sync.dma_start(out=res_sb[:], in_=res.rearrange("(p t) m -> p t m", t=PACK))
 
         neg_bias = sb("neg_bias", [P, PACK], F32)
@@ -96,11 +96,15 @@ def tile_attend_tcpairshare_o_pl_kernel(tc, tab_words, tab_scales, dtab_words, d
         w1_bf = sb("w1_bf", [P, PACK, P, PACK], BF16)
         w1_codes = sb("w1_codes", [P, R], U32)
         w1_scales = sb("w1_scales", [P, R], U8)
-        for h, copy in enumerate((nc.scalar.copy, nc.vector.tensor_copy)):
+        def round_w1(copy, h, m0, m1):
             copy(
-                w1_bf[:, :, h * (P // 2) : (h + 1) * (P // 2), :].rearrange("p t m j -> p m j t"),
-                w1_raw[h][:].rearrange("p j (m t) -> p m j t", t=PACK),
+                w1_bf[:, :, h * 64 + m0 : h * 64 + m1, :].rearrange("p t m j -> p m j t"),
+                w1_raw[h][:, :, PACK * m0 : PACK * m1].rearrange("p j (m t) -> p m j t", t=PACK),
             )
+
+        round_w1(nc.scalar.copy, 0, 0, 64)
+        round_w1(nc.vector.tensor_copy, 1, 0, 44)
+        round_w1(nc.scalar.copy, 1, 44, 64)
         a_ps = [psum.tile([P, J], F32, name="a_ps%d" % t) for t in range(PACK)]
         ta_ps = [psum.tile([P, J], F32, name="ta_ps%d" % t) for t in range(PACK)]
 
@@ -125,54 +129,97 @@ def tile_attend_tcpairshare_o_pl_kernel(tc, tab_words, tab_scales, dtab_words, d
         h1 = per_tile("h1", J)
         th1 = per_tile("th1", J)
         for t in range(PACK):
-            nc.scalar.activation(sig[t][:], a_ps[t][:], ACT.Sigmoid, bias=bias_sb[:, t : t + 1])
             nc.scalar.activation(sig_neg[t][:], a_ps[t][:], ACT.Sigmoid, bias=neg_bias[:, t : t + 1], scale=-1.0)
+            nc.gpsimd.tensor_scalar(sig[t][:], sig_neg[t][:], -1.0, 1.0, ALU.mult, ALU.add)
+        nc.vector.tensor_scalar(x[0][:], a_ps[0][:], bias_sb[:, 0:1], None, ALU.add)
         for t in range(PACK):
             nc.vector.tensor_tensor(th1[t][:], ta_ps[t][:], sig[t][:], ALU.mult)
-        nc.vector.tensor_scalar(x[0][:], a_ps[0][:], bias_sb[:, 0:1], None, ALU.add)
+        nc.gpsimd.tensor_scalar(half_c[:], reserve_sb[:], 0.5, 0.0, ALU.mult, ALU.add)
+        nc.gpsimd.tensor_tensor(c_rs[:], reserve_sb[:], rs_sb[:], ALU.mult)
+        nc.gpsimd.tensor_tensor(neg_quarter[:], c_rs[:], half_c[:], ALU.mult)
+        nc.gpsimd.tensor_scalar(neg_quarter[:], neg_quarter[:], -0.5, 0.0, ALU.mult, ALU.add)
+
+        ga = per_tile("ga", M)
+        gb = per_tile("gb", M)
+        dpart = per_tile("dpart", M)
+        d_abs = per_tile("d_abs", M)
+        sq = per_tile("sq", M)
+        u = per_tile("u", M)
+        num = sb("num", [P, PACK, M], F32)
+        d_log = sb("d_log", [P, PACK * M], F32)
+        inv_sq = sb("inv_sq", [P, PACK * M], F32)
+
+        for t in range(PACK):
+            if t > 0:
+                nc.scalar.activation(x[t][:], a_ps[t][:], ACT.Identity, bias=bias_sb[:, t : t + 1])
+            nc.scalar.activation(log_neg[t][:], sig_neg[t][:], ACT.Ln, bias=FLOOR)
+
+        def softplus(t):
+            nc.vector.scalar_tensor_tensor(h1[t][:], log_neg[t][:], -1.0, x[t][:], ALU.mult, ALU.max)
 
         wor_bf = sb("wor_bf", [P, PACK, P, PACK], BF16)
         wor_codes = sb("wor_codes", [P, F], U32)
         wor_scales = sb("wor_scales", [P, F], U8)
-        nc.vector.tensor_copy(wor_bf[:].rearrange("p t m j -> p m j t"), wor_raw[:].rearrange("p j (m t) -> p m j t", t=PACK))
-        nc.vector.quantize_mx(out=wor_codes[:].bitcast(FP8X4), scales=wor_scales[:], in_=wor_bf[:].rearrange("p t m j -> p (t m j)"))
 
-        nc.vector.tensor_scalar(half_c[:], reserve_sb[:], 0.5, None, ALU.mult)
-        nc.vector.tensor_tensor(c_rs[:], reserve_sb[:], rs_sb[:], ALU.mult)
-        nc.vector.scalar_tensor_tensor(neg_quarter[:], c_rs[:], -0.25, reserve_sb[:], ALU.mult, ALU.mult)
-        ga = per_tile("ga", M)
-        gb = per_tile("gb", M)
-        dpart = per_tile("dpart", M)
-        sq = per_tile("sq", M)
-        u = per_tile("u", M)
-        t1 = per_tile("t1", M)
-        t2 = per_tile("t2", M)
-        num = per_tile("num", M)
-        d_abs = sb("d_abs", [P, PACK * M], F32)
-        d_log = sb("d_log", [P, PACK * M], F32)
-        inv_sq = sb("inv_sq", [P, PACK * M], F32)
-        fo = sb("fo", [P, PACK, M], BF16)
+        def denominator_log(t):
+            nc.scalar.activation(d_abs[t][:], dpart[t][:], ACT.Abs, bias=reserve_sb[:, t : t + 1])
+            nc.scalar.activation(d_log[:, t * M : (t + 1) * M], d_abs[t][:], ACT.Ln)
 
-        for t in range(PACK):
-            nc.scalar.activation(log_neg[t][:], sig_neg[t][:], ACT.Ln, bias=FLOOR)
-            if t > 0:
-                nc.scalar.activation(x[t][:], a_ps[t][:], ACT.Identity, bias=bias_sb[:, t : t + 1])
-        for t in range(PACK):
-            nc.vector.scalar_tensor_tensor(h1[t][:], log_neg[t][:], -1.0, x[t][:], ALU.mult, ALU.max)
-            nc.vector.tensor_copy(ga[t][:], h1[t][:].indirect(first[:]))
-            nc.vector.tensor_copy(gb[t][:], h1[t][:].indirect(second[:]))
-            nc.vector.scalar_tensor_tensor(dpart[t][:], gb[t][:], 1.0, ga[t][:], ALU.add, ALU.mult)
-            nc.scalar.activation(d_abs[:, t * M : (t + 1) * M], dpart[t][:], ACT.Abs, bias=reserve_sb[:, t : t + 1])
-        nc.scalar.activation(d_log[:], d_abs[:], ACT.Ln)
-        nc.scalar.activation(inv_sq[:], d_log[:], ACT.Exp, scale=-2.0)
-        for t in range(PACK):
+        def first_factor(t):
             nc.scalar.activation(sq[t][:], ga[t][:], ACT.Square, bias=half_c[:, t : t + 1])
             nc.scalar.activation(u[t][:], sq[t][:], ACT.Identity, bias=neg_quarter[:, t : t + 1], scale=rs_sb[:, t : t + 1])
+
+        def round_wor(q):
+            nc.scalar.copy(
+                wor_bf[:, :, q * 32 : (q + 1) * 32, :].rearrange("p t m j -> p m j t"),
+                wor_raw[:, :, q * P : (q + 1) * P].rearrange("p j (m t) -> p m j t", t=PACK),
+            )
+
+        def denominator(t):
+            nc.vector.scalar_tensor_tensor(dpart[t][:], gb[t][:], 1.0, ga[t][:], ALU.add, ALU.mult)
+
+        def look_up_h1(t):
+            nc.vector.tensor_copy(ga[t][:], h1[t][:].indirect(first[:]))
+            nc.vector.tensor_copy(gb[t][:], h1[t][:].indirect(second[:]))
+
+        last = PACK - 1
+        softplus(0)
+        for t in range(last):
+            look_up_h1(t)
+            softplus(t + 1)
+            denominator(t)
+            first_factor(t)
+            denominator_log(t)
+            round_wor(t)
+
+        t1 = sb("t1", [P, PACK, M], F32, tag="x%d" % last)
+        t2 = sb("t2", [P, PACK, M], F32, tag="log_neg%d" % last)
+
+        def term2(t):
+            nc.vector.tensor_tensor(t2[:, t, :], th1[t][:].indirect(first[:]), gb[t][:], ALU.mult)
+
+        def term1(t):
+            nc.vector.tensor_tensor(t1[:, t, :], th1[t][:].indirect(second[:]), u[t][:], ALU.mult)
+
+        def numerator(t):
+            nc.vector.scalar_tensor_tensor(num[:, t, :], t2[:, t, :], c_rs[:, t : t + 1], t1[:, t, :], ALU.mult, ALU.add)
+
+        look_up_h1(last)
+        term2(0)
+        denominator(last)
+        first_factor(last)
+        denominator_log(last)
+        nc.scalar.activation(inv_sq[:], d_log[:], ACT.Exp, scale=-2.0)
+        round_wor(last)
+
         for t in range(PACK):
-            nc.vector.tensor_tensor(t2[t][:], th1[t][:].indirect(first[:]), gb[t][:], ALU.mult)
-            nc.vector.tensor_tensor(t1[t][:], th1[t][:].indirect(second[:]), u[t][:], ALU.mult)
-            nc.vector.scalar_tensor_tensor(num[t][:], t2[t][:], c_rs[:, t : t + 1], t1[t][:], ALU.mult, ALU.add)
-            nc.vector.tensor_tensor(fo[:, t, :], num[t][:], inv_sq[:, t * M : (t + 1) * M], ALU.mult)
+            term1(t)
+            if t + 1 < PACK:
+                term2(t + 1)
+            if t > 0:
+                numerator(t - 1)
+        numerator(last)
+        nc.vector.quantize_mx(out=wor_codes[:].bitcast(FP8X4), scales=wor_scales[:], in_=wor_bf[:].rearrange("p t m j -> p (t m j)"))
 
         y_codes = sb("y_codes", [P, M], U32)
         y_scales = sb("y_scales", [P, M], U8)
@@ -188,8 +235,14 @@ def tile_attend_tcpairshare_o_pl_kernel(tc, tab_words, tab_scales, dtab_words, d
         y = [sb("y%d" % h, [P, PACK, HALF], F32) for h in range(2)]
         y_il = [sb("y_il%d" % h, [P, HALF, PACK], BF16) for h in range(2)]
         halves = [slice(h * HALF, (h + 1) * HALF) for h in range(2)]
-        interleave(nc.vector.tensor_copy, fo_il[0][:], fo[:, :, halves[0]])
-        interleave(nc.scalar.copy, fo_il[1][:], fo[:, :, halves[1]])
+        inv_sq_tiles = inv_sq[:].rearrange("p (t m) -> p t m", t=PACK)
+        for h in range(2):
+            nc.vector.tensor_tensor(
+                fo_il[h][:].rearrange("p (c i) t -> p c t i", i=4),
+                num[:, :, halves[h]].rearrange("p t (c i) -> p c t i", i=4),
+                inv_sq_tiles[:, :, halves[h]].rearrange("p t (c i) -> p c t i", i=4),
+                ALU.mult,
+            )
         yo_ps = []
         for h in range(2):
             nc.vector.quantize_mx(out=fo_codes[h][:].bitcast(FP8X4), scales=fo_scales[h][:], in_=fo_il[h][:].rearrange("p m t -> p (m t)"))
@@ -201,9 +254,15 @@ def tile_attend_tcpairshare_o_pl_kernel(tc, tab_words, tab_scales, dtab_words, d
         for h in range(2):
             nc.vector.tensor_tensor(y[h][:], yo_ps[h][:].rearrange("p (t m) -> p t m", t=PACK), res_sb[:, :, halves[h]], ALU.add)
             nc.sync.dma_start(out=out_rows[:, :, halves[h]], in_=y[h][:])
-            interleave(nc.scalar.copy, y_il[h][:], y[h][:])
-        for h in range(2):
+
+        def quantize_y(h):
             nc.vector.quantize_mx(out=y_codes[:, halves[h]].bitcast(FP8X4), scales=y_scales[:, halves[h]], in_=y_il[h][:].rearrange("p m t -> p (m t)"))
-        nc.sync.dma_start(out=out_words, in_=y_codes[:].bitcast(I32))
-        for q in range(4):
-            nc.sync.dma_start(out=out_2[0, 4 * q : 4 * q + 4, :].bitcast(I32), in_=y_scales[32 * q : 32 * q + 4, :].bitcast(I32))
+            nc.sync.dma_start(out=out_words[:, halves[h]], in_=y_codes[:, halves[h]].bitcast(I32))
+
+        interleave(nc.scalar.copy, y_il[0][:], y[0][:])
+        interleave(nc.scalar.copy, y_il[1][:, :48, :], y[1][:, :, :48])
+        interleave(nc.vector.tensor_copy, y_il[1][:, 48:, :], y[1][:, :, 48:])
+        quantize_y(0)
+        quantize_y(1)
+        for q, queue in enumerate((nc.scalar, nc.scalar, nc.sync, nc.sync)):
+            queue.dma_start(out=out_2[0, 4 * q : 4 * q + 4, :].bitcast(I32), in_=y_scales[32 * q : 32 * q + 4, :].bitcast(I32))

@@ -3,7 +3,7 @@ from contextlib import ExitStack
 import concourse.mybir as mybir
 
 K, R, F, T, J, M = 512, 512, 512, 2048, 512, 256
-FLOPS = 2 * K * R * J * 2 + 2 * R * F * M
+FLOPS = 2 * (2 * K * R * J) + 2 * R * F * M
 
 F32 = mybir.dt.float32
 BF16 = mybir.dt.bfloat16
@@ -18,8 +18,14 @@ ACT = mybir.ActivationFunctionType
 
 P = 128
 PACK = 4
+LAST = PACK - 1
+QUADRANTS = 4
+LINE = 4
 HALF = M // 2
-FLOOR = 2.0**-60
+FLOOR_AT = -40.0
+W1_PLACES = P // 2
+W1_VECTOR_PLACES = 44
+Y_SCALAR_COLUMNS = 48
 
 
 def tile_attend_tcpairshare_o_pl_kernel(tc, tab_words, tab_scales, dtab_words, dtab_scales, w1, bias, reserve, rs, wor, res, offs, offs2, offs3, out_0, out_1, out_2):
@@ -29,11 +35,14 @@ def tile_attend_tcpairshare_o_pl_kernel(tc, tab_words, tab_scales, dtab_words, d
         keep = ctx.enter_context(tc.tile_pool(name="keep", bufs=1))
         psum = ctx.enter_context(tc.psum_pool(name="psum", bufs=1))
 
-        def sb(name, shape, dtype, tag=None):
-            return keep.tile(shape, dtype, name=name, tag=tag or name, align_bytes=64)
+        def sb(name, shape, dtype, after=None):
+            return keep.tile(shape, dtype, name=name, tag=after or name, align_bytes=64)
 
-        def per_tile(name, width, dtype=F32):
-            return [sb("%s%d" % (name, t), [P, width], dtype) for t in range(PACK)]
+        def per_deal(name, width):
+            return [sb("%s%d" % (name, t), [P, width], F32) for t in range(PACK)]
+
+        def deal(t):
+            return slice(t * P, (t + 1) * P)
 
         slots = lists.tile([P, J // 16], U16, name="slots")
         first = lists.tile([P, M // 16], U16, name="first")
@@ -50,16 +59,18 @@ def tile_attend_tcpairshare_o_pl_kernel(tc, tab_words, tab_scales, dtab_words, d
         reserve_sb = sb("reserve_sb", [P, PACK], F32)
         rs_sb = sb("rs_sb", [P, PACK], F32)
 
-        def load_scales(tile, scales):
-            for q in range(4):
-                nc.sync.dma_start(out=tile[32 * q : 32 * q + 4, :].bitcast(I32), in_=scales[0, 4 * q : 4 * q + 4, :].bitcast(I32))
-
         nc.vector.memset(tab_s[:].bitcast(I32), 0)
         nc.vector.memset(dtab_s[:].bitcast(I32), 0)
-        warm = sb("warm", [P, 1], F32)
-        warm_out = sb("warm_out", [P, 1], F32)
-        nc.vector.memset(warm[:], 0.0)
-        nc.scalar.activation(warm_out[:], warm[:], ACT.Sigmoid)
+        floor_at = sb("floor_at", [P, 1], F32)
+        floor = sb("floor", [P, 1], F32)
+        nc.vector.memset(floor_at[:], FLOOR_AT)
+        one = sb("one", [P, 1], F32)
+        nc.vector.memset(one[:], 1.0)
+        nc.scalar.activation(floor[:], floor_at[:], ACT.Sigmoid)
+
+        def load_scales(tile, scales):
+            for q in range(QUADRANTS):
+                nc.sync.dma_start(out=tile[32 * q : 32 * q + 4, :].bitcast(I32), in_=scales[0, 4 * q : 4 * q + 4, :].bitcast(I32))
 
         def load_column(tile, column):
             nc.sync.dma_start(out=tile[:], in_=column.rearrange("(p t) o -> p (t o)", t=PACK))
@@ -81,9 +92,6 @@ def tile_attend_tcpairshare_o_pl_kernel(tc, tab_words, tab_scales, dtab_words, d
         nc.sync.dma_start(out=res_sb[:], in_=res.rearrange("(p t) m -> p t m", t=PACK))
 
         neg_bias = sb("neg_bias", [P, PACK], F32)
-        half_c = sb("half_c", [P, PACK], F32)
-        c_rs = sb("c_rs", [P, PACK], F32)
-        neg_quarter = sb("neg_quarter", [P, PACK], F32)
         nc.scalar.activation(neg_bias[:], bias_sb[:], ACT.Copy, scale=-1.0)
 
         tab_gw = sb("tab_gw", [P, J], U16)
@@ -93,28 +101,27 @@ def tile_attend_tcpairshare_o_pl_kernel(tc, tab_words, tab_scales, dtab_words, d
         nc.vector.tensor_copy(tab_gw[:], tab_w[:].indirect(slots[:]))
         nc.vector.tensor_copy(tab_gs[:], tab_s[:].indirect(slots[:]))
 
+        def round_and_deal(copy, dealt, raw):
+            copy(dealt.rearrange("p t n j -> p n j t"), raw.rearrange("p j (n t) -> p n j t", t=PACK))
+
         w1_bf = sb("w1_bf", [P, PACK, P, PACK], BF16)
         w1_codes = sb("w1_codes", [P, R], U32)
         w1_scales = sb("w1_scales", [P, R], U8)
-        def round_w1(copy, h, m0, m1):
-            copy(
-                w1_bf[:, :, h * 64 + m0 : h * 64 + m1, :].rearrange("p t m j -> p m j t"),
-                w1_raw[h][:, :, PACK * m0 : PACK * m1].rearrange("p j (m t) -> p m j t", t=PACK),
-            )
 
-        round_w1(nc.scalar.copy, 0, 0, 64)
-        round_w1(nc.vector.tensor_copy, 1, 0, 44)
-        round_w1(nc.scalar.copy, 1, 44, 64)
+        def round_w1(copy, h, n0, n1):
+            round_and_deal(copy, w1_bf[:, :, h * W1_PLACES + n0 : h * W1_PLACES + n1, :], w1_raw[h][:, :, PACK * n0 : PACK * n1])
+
+        round_w1(nc.scalar.copy, 0, 0, W1_PLACES)
+        round_w1(nc.vector.tensor_copy, 1, 0, W1_VECTOR_PLACES)
+        round_w1(nc.scalar.copy, 1, W1_VECTOR_PLACES, W1_PLACES)
         a_ps = [psum.tile([P, J], F32, name="a_ps%d" % t) for t in range(PACK)]
         ta_ps = [psum.tile([P, J], F32, name="ta_ps%d" % t) for t in range(PACK)]
 
         def first_layer(bank, t, words, scales):
-            cols = slice(t * P, (t + 1) * P)
-            nc.tensor.matmul_mx(out=bank[:], lhsT=w1_codes[:, cols].bitcast(FP8X4), lhsT_scale=w1_scales[:, cols], rhs=words[:].bitcast(FP4X4), rhs_scale=scales[:], start=True, stop=True)
+            nc.tensor.matmul_mx(out=bank[:], lhsT=w1_codes[:, deal(t)].bitcast(FP8X4), lhsT_scale=w1_scales[:, deal(t)], rhs=words[:].bitcast(FP4X4), rhs_scale=scales[:], start=True, stop=True)
 
         for t in range(PACK):
-            cols = slice(t * P, (t + 1) * P)
-            nc.vector.quantize_mx(out=w1_codes[:, cols].bitcast(FP8X4), scales=w1_scales[:, cols], in_=w1_bf[:, t, :, :].rearrange("p m j -> p (m j)"))
+            nc.vector.quantize_mx(out=w1_codes[:, deal(t)].bitcast(FP8X4), scales=w1_scales[:, deal(t)], in_=w1_bf[:, t, :, :].rearrange("p n j -> p (n j)"))
             first_layer(a_ps[t], t, tab_gw, tab_gs)
 
         nc.vector.tensor_copy(dtab_gw[:], dtab_w[:].indirect(slots[:]))
@@ -122,69 +129,71 @@ def tile_attend_tcpairshare_o_pl_kernel(tc, tab_words, tab_scales, dtab_words, d
         for t in range(PACK):
             first_layer(ta_ps[t], t, dtab_gw, dtab_gs)
 
-        sig = per_tile("sig", J)
-        sig_neg = per_tile("sig_neg", J)
-        x = per_tile("x", J)
-        log_neg = per_tile("log_neg", J)
-        h1 = per_tile("h1", J)
-        th1 = per_tile("th1", J)
+        sig_neg = per_deal("sig_neg", J)
+        front = sb("front", [P, 2, J], F32, after="dtab_s")
+        x = [front[:, 1, :]] + [sb("x%d" % t, [P, J], F32)[:] for t in range(1, PACK)]
+        log_neg = per_deal("log_neg", J)
+        h1 = per_deal("h1", J)
+        th1 = per_deal("th1", J)
         for t in range(PACK):
             nc.scalar.activation(sig_neg[t][:], a_ps[t][:], ACT.Sigmoid, bias=neg_bias[:, t : t + 1], scale=-1.0)
-            nc.gpsimd.tensor_scalar(sig[t][:], sig_neg[t][:], -1.0, 1.0, ALU.mult, ALU.add)
-        nc.vector.tensor_scalar(x[0][:], a_ps[0][:], bias_sb[:, 0:1], None, ALU.add)
+        nc.vector.tensor_scalar(front[:, 0, :], sig_neg[0][:], -1.0, one[:], ALU.mult, ALU.add)
+        sig_rest = sb("sig_rest", [P, LAST, J], F32, after="one")
+        sig = [front[:, 0, :]] + [sig_rest[:, t - 1, :] for t in range(1, PACK)]
+        for t in range(1, PACK):
+            nc.gpsimd.tensor_scalar(sig[t], sig_neg[t][:], -1.0, 1.0, ALU.mult, ALU.add)
+        nc.vector.tensor_scalar(x[0], a_ps[0][:], bias_sb[:, 0:1], None, ALU.add)
         for t in range(PACK):
-            nc.vector.tensor_tensor(th1[t][:], ta_ps[t][:], sig[t][:], ALU.mult)
-        nc.gpsimd.tensor_scalar(half_c[:], reserve_sb[:], 0.5, 0.0, ALU.mult, ALU.add)
-        nc.gpsimd.tensor_tensor(c_rs[:], reserve_sb[:], rs_sb[:], ALU.mult)
-        nc.gpsimd.tensor_tensor(neg_quarter[:], c_rs[:], half_c[:], ALU.mult)
-        nc.gpsimd.tensor_scalar(neg_quarter[:], neg_quarter[:], -0.5, 0.0, ALU.mult, ALU.add)
+            nc.vector.tensor_tensor(th1[t][:], ta_ps[t][:], sig[t], ALU.mult)
+        factors = sb("factors", [P, 3, PACK], F32, after="one")
+        c_rs, half_c, neg_quarter = (factors[:, i, :] for i in range(3))
+        nc.vector.tensor_tensor(c_rs, reserve_sb[:], rs_sb[:], ALU.mult)
+        nc.vector.tensor_scalar(half_c, reserve_sb[:], 0.5, None, ALU.mult)
+        nc.vector.scalar_tensor_tensor(neg_quarter, c_rs, -0.25, reserve_sb[:], ALU.mult, ALU.mult)
 
-        ga = per_tile("ga", M)
-        gb = per_tile("gb", M)
-        dpart = per_tile("dpart", M)
-        d_abs = per_tile("d_abs", M)
-        sq = per_tile("sq", M)
-        u = per_tile("u", M)
+        look_a = per_deal("look_a", M)
+        look_b = per_deal("look_b", M)
+        d_part = per_deal("d_part", M)
+        d_abs = per_deal("d_abs", M)
+        square = per_deal("square", M)
+        u = per_deal("u", M)
         num = sb("num", [P, PACK, M], F32)
         d_log = sb("d_log", [P, PACK * M], F32)
         inv_sq = sb("inv_sq", [P, PACK * M], F32)
 
         for t in range(PACK):
             if t > 0:
-                nc.scalar.activation(x[t][:], a_ps[t][:], ACT.Identity, bias=bias_sb[:, t : t + 1])
-            nc.scalar.activation(log_neg[t][:], sig_neg[t][:], ACT.Ln, bias=FLOOR)
+                nc.scalar.activation(x[t], a_ps[t][:], ACT.Identity, bias=bias_sb[:, t : t + 1])
+            nc.scalar.activation(log_neg[t][:], sig_neg[t][:], ACT.Ln, bias=floor[:])
 
         def softplus(t):
-            nc.vector.scalar_tensor_tensor(h1[t][:], log_neg[t][:], -1.0, x[t][:], ALU.mult, ALU.max)
+            nc.vector.scalar_tensor_tensor(h1[t][:], log_neg[t][:], -1.0, x[t], ALU.mult, ALU.max)
 
         wor_bf = sb("wor_bf", [P, PACK, P, PACK], BF16)
         wor_codes = sb("wor_codes", [P, F], U32)
         wor_scales = sb("wor_scales", [P, F], U8)
 
         def denominator_log(t):
-            nc.scalar.activation(d_abs[t][:], dpart[t][:], ACT.Abs, bias=reserve_sb[:, t : t + 1])
+            nc.scalar.activation(d_abs[t][:], d_part[t][:], ACT.Abs, bias=reserve_sb[:, t : t + 1])
             nc.scalar.activation(d_log[:, t * M : (t + 1) * M], d_abs[t][:], ACT.Ln)
 
         def first_factor(t):
-            nc.scalar.activation(sq[t][:], ga[t][:], ACT.Square, bias=half_c[:, t : t + 1])
-            nc.scalar.activation(u[t][:], sq[t][:], ACT.Identity, bias=neg_quarter[:, t : t + 1], scale=rs_sb[:, t : t + 1])
+            nc.scalar.activation(square[t][:], look_a[t][:], ACT.Square, bias=half_c[:, t : t + 1])
+            nc.scalar.activation(u[t][:], square[t][:], ACT.Identity, bias=neg_quarter[:, t : t + 1], scale=rs_sb[:, t : t + 1])
 
-        def round_wor(q):
-            nc.scalar.copy(
-                wor_bf[:, :, q * 32 : (q + 1) * 32, :].rearrange("p t m j -> p m j t"),
-                wor_raw[:, :, q * P : (q + 1) * P].rearrange("p j (m t) -> p m j t", t=PACK),
-            )
+        def round_wor(quarter):
+            places = P // PACK
+            round_and_deal(nc.scalar.copy, wor_bf[:, :, quarter * places : (quarter + 1) * places, :], wor_raw[:, :, quarter * P : (quarter + 1) * P])
 
         def denominator(t):
-            nc.vector.scalar_tensor_tensor(dpart[t][:], gb[t][:], 1.0, ga[t][:], ALU.add, ALU.mult)
+            nc.vector.scalar_tensor_tensor(d_part[t][:], look_b[t][:], 1.0, look_a[t][:], ALU.add, ALU.mult)
 
         def look_up_h1(t):
-            nc.vector.tensor_copy(ga[t][:], h1[t][:].indirect(first[:]))
-            nc.vector.tensor_copy(gb[t][:], h1[t][:].indirect(second[:]))
+            nc.vector.tensor_copy(look_a[t][:], h1[t][:].indirect(first[:]))
+            nc.vector.tensor_copy(look_b[t][:], h1[t][:].indirect(second[:]))
 
-        last = PACK - 1
         softplus(0)
-        for t in range(last):
+        for t in range(LAST):
             look_up_h1(t)
             softplus(t + 1)
             denominator(t)
@@ -192,77 +201,84 @@ def tile_attend_tcpairshare_o_pl_kernel(tc, tab_words, tab_scales, dtab_words, d
             denominator_log(t)
             round_wor(t)
 
-        t1 = sb("t1", [P, PACK, M], F32, tag="x%d" % last)
-        t2 = sb("t2", [P, PACK, M], F32, tag="log_neg%d" % last)
+        term_b = sb("term_b", [P, PACK, M], F32, after="x%d" % LAST)
+        term_a = sb("term_a", [P, PACK, M], F32, after="log_neg%d" % LAST)
 
-        def term2(t):
-            nc.vector.tensor_tensor(t2[:, t, :], th1[t][:].indirect(first[:]), gb[t][:], ALU.mult)
+        def make_term_a(t):
+            nc.vector.tensor_tensor(term_a[:, t, :], th1[t][:].indirect(first[:]), look_b[t][:], ALU.mult)
 
-        def term1(t):
-            nc.vector.tensor_tensor(t1[:, t, :], th1[t][:].indirect(second[:]), u[t][:], ALU.mult)
+        def make_term_b(t):
+            nc.vector.tensor_tensor(term_b[:, t, :], th1[t][:].indirect(second[:]), u[t][:], ALU.mult)
 
-        def numerator(t):
-            nc.vector.scalar_tensor_tensor(num[:, t, :], t2[:, t, :], c_rs[:, t : t + 1], t1[:, t, :], ALU.mult, ALU.add)
+        def numerator(t, cols):
+            nc.vector.scalar_tensor_tensor(num[:, t, cols], term_a[:, t, cols], c_rs[:, t : t + 1], term_b[:, t, cols], ALU.mult, ALU.add)
 
-        look_up_h1(last)
-        term2(0)
-        denominator(last)
-        first_factor(last)
-        denominator_log(last)
+        look_up_h1(LAST)
+        make_term_a(0)
+        denominator(LAST)
+        first_factor(LAST)
+        denominator_log(LAST)
         nc.scalar.activation(inv_sq[:], d_log[:], ACT.Exp, scale=-2.0)
-        round_wor(last)
+        round_wor(LAST)
 
         for t in range(PACK):
-            term1(t)
-            if t + 1 < PACK:
-                term2(t + 1)
+            make_term_b(t)
+            if t < LAST:
+                make_term_a(t + 1)
             if t > 0:
-                numerator(t - 1)
-        numerator(last)
-        nc.vector.quantize_mx(out=wor_codes[:].bitcast(FP8X4), scales=wor_scales[:], in_=wor_bf[:].rearrange("p t m j -> p (t m j)"))
+                numerator(t - 1, slice(0, M))
 
         y_codes = sb("y_codes", [P, M], U32)
         y_scales = sb("y_scales", [P, M], U8)
         out_rows = out_0.rearrange("(p t) m -> p t m", t=PACK)
         out_words = out_1[0].rearrange("p m t -> p (m t)").bitcast(I32)
 
-        def interleave(copy, dst, src):
-            copy(dst.rearrange("p (c i) t -> p c t i", i=4), src.rearrange("p t (c i) -> p c t i", i=4))
+        def by_deal(ap):
+            return ap.rearrange("p t (c i) -> p c t i", i=LINE)
 
-        fo_il = [sb("fo_il%d" % h, [P, HALF, PACK], BF16) for h in range(2)]
+        def by_word(ap):
+            return ap.rearrange("p (c i) t -> p c t i", i=LINE)
+
+        fo_bf = [sb("fo_bf%d" % h, [P, HALF, PACK], BF16) for h in range(2)]
         fo_codes = [sb("fo_codes%d" % h, [P, HALF], U32) for h in range(2)]
         fo_scales = [sb("fo_scales%d" % h, [P, HALF], U8) for h in range(2)]
         y = [sb("y%d" % h, [P, PACK, HALF], F32) for h in range(2)]
-        y_il = [sb("y_il%d" % h, [P, HALF, PACK], BF16) for h in range(2)]
+        y_bf = [sb("y_bf%d" % h, [P, HALF, PACK], BF16) for h in range(2)]
         halves = [slice(h * HALF, (h + 1) * HALF) for h in range(2)]
-        inv_sq_tiles = inv_sq[:].rearrange("p (t m) -> p t m", t=PACK)
-        for h in range(2):
-            nc.vector.tensor_tensor(
-                fo_il[h][:].rearrange("p (c i) t -> p c t i", i=4),
-                num[:, :, halves[h]].rearrange("p t (c i) -> p c t i", i=4),
-                inv_sq_tiles[:, :, halves[h]].rearrange("p t (c i) -> p c t i", i=4),
-                ALU.mult,
-            )
-        yo_ps = []
-        for h in range(2):
-            nc.vector.quantize_mx(out=fo_codes[h][:].bitcast(FP8X4), scales=fo_scales[h][:], in_=fo_il[h][:].rearrange("p m t -> p (m t)"))
-            bank = psum.tile([P, J], F32, name="a_ps%d" % h)
-            yo_ps.append(bank)
+        inv_sq_deals = inv_sq[:].rearrange("p (t m) -> p t m", t=PACK)
+
+        def quotient(h):
+            nc.vector.tensor_tensor(by_word(fo_bf[h][:]), by_deal(num[:, :, halves[h]]), by_deal(inv_sq_deals[:, :, halves[h]]), ALU.mult)
+
+        def last_layer(h):
+            nc.vector.quantize_mx(out=fo_codes[h][:].bitcast(FP8X4), scales=fo_scales[h][:], in_=fo_bf[h][:].rearrange("p m t -> p (m t)"))
+            bank = psum.tile([P, PACK * HALF], F32, name="ta_ps%d" % h)
             for t in range(PACK):
-                cols = slice(t * P, (t + 1) * P)
-                nc.tensor.matmul_mx(out=bank[:, t * HALF : (t + 1) * HALF], lhsT=wor_codes[:, cols].bitcast(FP8X4), lhsT_scale=wor_scales[:, cols], rhs=fo_codes[h][:].bitcast(FP8X4), rhs_scale=fo_scales[h][:], start=True, stop=True)
+                nc.tensor.matmul_mx(out=bank[:, t * HALF : (t + 1) * HALF], lhsT=wor_codes[:, deal(t)].bitcast(FP8X4), lhsT_scale=wor_scales[:, deal(t)], rhs=fo_codes[h][:].bitcast(FP8X4), rhs_scale=fo_scales[h][:], start=True, stop=True)
+            return bank
+
+        numerator(LAST, halves[0])
+        numerator(LAST, halves[1])
+        quotient(0)
+        nc.vector.quantize_mx(out=wor_codes[:].bitcast(FP8X4), scales=wor_scales[:], in_=wor_bf[:].rearrange("p t n j -> p (t n j)"))
+        yo_ps = [last_layer(0)]
+        quotient(1)
+        yo_ps.append(last_layer(1))
         for h in range(2):
             nc.vector.tensor_tensor(y[h][:], yo_ps[h][:].rearrange("p (t m) -> p t m", t=PACK), res_sb[:, :, halves[h]], ALU.add)
             nc.sync.dma_start(out=out_rows[:, :, halves[h]], in_=y[h][:])
 
+        def round_y(copy, h, cols):
+            copy(by_word(y_bf[h][:, cols, :]), by_deal(y[h][:, :, cols]))
+
         def quantize_y(h):
-            nc.vector.quantize_mx(out=y_codes[:, halves[h]].bitcast(FP8X4), scales=y_scales[:, halves[h]], in_=y_il[h][:].rearrange("p m t -> p (m t)"))
+            nc.vector.quantize_mx(out=y_codes[:, halves[h]].bitcast(FP8X4), scales=y_scales[:, halves[h]], in_=y_bf[h][:].rearrange("p m t -> p (m t)"))
             nc.sync.dma_start(out=out_words[:, halves[h]], in_=y_codes[:, halves[h]].bitcast(I32))
 
-        interleave(nc.scalar.copy, y_il[0][:], y[0][:])
-        interleave(nc.scalar.copy, y_il[1][:, :48, :], y[1][:, :, :48])
-        interleave(nc.vector.tensor_copy, y_il[1][:, 48:, :], y[1][:, :, 48:])
+        round_y(nc.scalar.copy, 0, slice(0, HALF))
+        round_y(nc.scalar.copy, 1, slice(0, Y_SCALAR_COLUMNS))
         quantize_y(0)
+        round_y(nc.vector.tensor_copy, 1, slice(Y_SCALAR_COLUMNS, HALF))
         quantize_y(1)
         for q, queue in enumerate((nc.scalar, nc.scalar, nc.sync, nc.sync)):
             queue.dma_start(out=out_2[0, 4 * q : 4 * q + 4, :].bitcast(I32), in_=y_scales[32 * q : 32 * q + 4, :].bitcast(I32))

from contextlib import ExitStack

import concourse.mybir as mybir

K, R, F, T, J, M = 512, 512, 512, 2048, 512, 256
FLOPS = 2 * (2 * K * R * J) + 2 * R * F * M

F32 = mybir.dt.float32
BF16 = mybir.dt.bfloat16
I32 = mybir.dt.int32
U32 = mybir.dt.uint32
U16 = mybir.dt.uint16
U8 = mybir.dt.uint8
FP8X4 = mybir.dt.float8_e4m3fn_x4
FP4X4 = mybir.dt.float4_e2m1fn_x4
ALU = mybir.AluOpType
ACT = mybir.ActivationFunctionType

P = 128
PACK = 4
LAST = PACK - 1
QUADRANTS = 4
LINE = 4
HALF = M // 2
FLOOR_AT = -40.0
W1_PLACES = P // 2
W1_VECTOR_PLACES = 44
Y_SCALAR_COLUMNS = 48


def tile_attend_tcpairshare_o_pl_kernel(tc, tab_words, tab_scales, dtab_words, dtab_scales, w1, bias, reserve, rs, wor, res, offs, offs2, offs3, out_0, out_1, out_2):
    nc = tc.nc
    with ExitStack() as ctx:
        lists = ctx.enter_context(tc.tile_pool(name="lists", bufs=1))
        keep = ctx.enter_context(tc.tile_pool(name="keep", bufs=1))
        psum = ctx.enter_context(tc.psum_pool(name="psum", bufs=1))

        def sb(name, shape, dtype, after=None):
            return keep.tile(shape, dtype, name=name, tag=after or name, align_bytes=64)

        def per_deal(name, width):
            return [sb("%s%d" % (name, t), [P, width], F32) for t in range(PACK)]

        def deal(t):
            return slice(t * P, (t + 1) * P)

        slots = lists.tile([P, J // 16], U16, name="slots")
        first = lists.tile([P, M // 16], U16, name="first")
        second = lists.tile([P, M // 16], U16, name="second")

        tab_w = sb("tab_w", [P, T], U16)
        tab_s = sb("tab_s", [P, T], U8)
        dtab_w = sb("dtab_w", [P, T], U16)
        dtab_s = sb("dtab_s", [P, T], U8)
        w1_raw = [sb("w1_raw%d" % h, [P, PACK, R // 2], F32) for h in range(2)]
        wor_raw = sb("wor_raw", [P, PACK, F], F32)
        res_sb = sb("res_sb", [P, PACK, M], F32)
        bias_sb = sb("bias_sb", [P, PACK], F32)
        reserve_sb = sb("reserve_sb", [P, PACK], F32)
        rs_sb = sb("rs_sb", [P, PACK], F32)

        nc.vector.memset(tab_s[:].bitcast(I32), 0)
        nc.vector.memset(dtab_s[:].bitcast(I32), 0)
        floor_at = sb("floor_at", [P, 1], F32)
        floor = sb("floor", [P, 1], F32)
        nc.vector.memset(floor_at[:], FLOOR_AT)
        one = sb("one", [P, 1], F32)
        nc.vector.memset(one[:], 1.0)
        nc.scalar.activation(floor[:], floor_at[:], ACT.Sigmoid)

        def load_scales(tile, scales):
            for q in range(QUADRANTS):
                nc.sync.dma_start(out=tile[32 * q : 32 * q + 4, :].bitcast(I32), in_=scales[0, 4 * q : 4 * q + 4, :].bitcast(I32))

        def load_column(tile, column):
            nc.sync.dma_start(out=tile[:], in_=column.rearrange("(p t) o -> p (t o)", t=PACK))

        nc.sync.dma_start(slots[:], offs)
        nc.sync.dma_start(out=tab_w[:].bitcast(I32), in_=tab_words[0].bitcast(I32))
        load_scales(tab_s, tab_scales)
        w1_rows = w1.rearrange("(p j) c -> p j c", j=PACK)
        for h in range(2):
            nc.sync.dma_start(out=w1_raw[h][:], in_=w1_rows[:, :, h * (R // 2) : (h + 1) * (R // 2)])
        load_column(bias_sb, bias)
        nc.sync.dma_start(out=dtab_w[:].bitcast(I32), in_=dtab_words[0].bitcast(I32))
        load_scales(dtab_s, dtab_scales)
        nc.sync.dma_start(first[:], offs2)
        nc.sync.dma_start(second[:], offs3)
        load_column(reserve_sb, reserve)
        load_column(rs_sb, rs)
        nc.sync.dma_start(out=wor_raw[:], in_=wor.rearrange("(p j) c -> p j c", j=PACK))
        nc.sync.dma_start(out=res_sb[:], in_=res.rearrange("(p t) m -> p t m", t=PACK))

        neg_bias = sb("neg_bias", [P, PACK], F32)
        nc.scalar.activation(neg_bias[:], bias_sb[:], ACT.Copy, scale=-1.0)

        tab_gw = sb("tab_gw", [P, J], U16)
        tab_gs = sb("tab_gs", [P, J], U8)
        dtab_gw = sb("dtab_gw", [P, J], U16)
        dtab_gs = sb("dtab_gs", [P, J], U8)
        nc.vector.tensor_copy(tab_gw[:], tab_w[:].indirect(slots[:]))
        nc.vector.tensor_copy(tab_gs[:], tab_s[:].indirect(slots[:]))

        def round_and_deal(copy, dealt, raw):
            copy(dealt.rearrange("p t n j -> p n j t"), raw.rearrange("p j (n t) -> p n j t", t=PACK))

        w1_bf = sb("w1_bf", [P, PACK, P, PACK], BF16)
        w1_codes = sb("w1_codes", [P, R], U32)
        w1_scales = sb("w1_scales", [P, R], U8)

        def round_w1(copy, h, n0, n1):
            round_and_deal(copy, w1_bf[:, :, h * W1_PLACES + n0 : h * W1_PLACES + n1, :], w1_raw[h][:, :, PACK * n0 : PACK * n1])

        round_w1(nc.scalar.copy, 0, 0, W1_PLACES)
        round_w1(nc.vector.tensor_copy, 1, 0, W1_VECTOR_PLACES)
        round_w1(nc.scalar.copy, 1, W1_VECTOR_PLACES, W1_PLACES)
        a_ps = [psum.tile([P, J], F32, name="a_ps%d" % t) for t in range(PACK)]
        ta_ps = [psum.tile([P, J], F32, name="ta_ps%d" % t) for t in range(PACK)]

        def first_layer(bank, t, words, scales):
            nc.tensor.matmul_mx(out=bank[:], lhsT=w1_codes[:, deal(t)].bitcast(FP8X4), lhsT_scale=w1_scales[:, deal(t)], rhs=words[:].bitcast(FP4X4), rhs_scale=scales[:], start=True, stop=True)

        for t in range(PACK):
            nc.vector.quantize_mx(out=w1_codes[:, deal(t)].bitcast(FP8X4), scales=w1_scales[:, deal(t)], in_=w1_bf[:, t, :, :].rearrange("p n j -> p (n j)"))
            first_layer(a_ps[t], t, tab_gw, tab_gs)

        nc.vector.tensor_copy(dtab_gw[:], dtab_w[:].indirect(slots[:]))
        nc.vector.tensor_copy(dtab_gs[:], dtab_s[:].indirect(slots[:]))
        for t in range(PACK):
            first_layer(ta_ps[t], t, dtab_gw, dtab_gs)

        sig_neg = per_deal("sig_neg", J)
        front = sb("front", [P, 2, J], F32, after="dtab_s")
        x = [front[:, 1, :]] + [sb("x%d" % t, [P, J], F32)[:] for t in range(1, PACK)]
        log_neg = per_deal("log_neg", J)
        h1 = per_deal("h1", J)
        th1 = per_deal("th1", J)
        for t in range(PACK):
            nc.scalar.activation(sig_neg[t][:], a_ps[t][:], ACT.Sigmoid, bias=neg_bias[:, t : t + 1], scale=-1.0)
        nc.vector.tensor_scalar(front[:, 0, :], sig_neg[0][:], -1.0, one[:], ALU.mult, ALU.add)
        sig_rest = sb("sig_rest", [P, LAST, J], F32, after="one")
        sig = [front[:, 0, :]] + [sig_rest[:, t - 1, :] for t in range(1, PACK)]
        for t in range(1, PACK):
            nc.gpsimd.tensor_scalar(sig[t], sig_neg[t][:], -1.0, 1.0, ALU.mult, ALU.add)
        nc.vector.tensor_scalar(x[0], a_ps[0][:], bias_sb[:, 0:1], None, ALU.add)
        for t in range(PACK):
            nc.vector.tensor_tensor(th1[t][:], ta_ps[t][:], sig[t], ALU.mult)
        factors = sb("factors", [P, 3, PACK], F32, after="one")
        c_rs, half_c, neg_quarter = (factors[:, i, :] for i in range(3))
        nc.vector.tensor_tensor(c_rs, reserve_sb[:], rs_sb[:], ALU.mult)
        nc.vector.tensor_scalar(half_c, reserve_sb[:], 0.5, None, ALU.mult)
        nc.vector.scalar_tensor_tensor(neg_quarter, c_rs, -0.25, reserve_sb[:], ALU.mult, ALU.mult)

        look_a = per_deal("look_a", M)
        look_b = per_deal("look_b", M)
        d_part = per_deal("d_part", M)
        d_abs = per_deal("d_abs", M)
        square = per_deal("square", M)
        u = per_deal("u", M)
        num = sb("num", [P, PACK, M], F32)
        d_log = sb("d_log", [P, PACK * M], F32)
        inv_sq = sb("inv_sq", [P, PACK * M], F32)

        for t in range(PACK):
            if t > 0:
                nc.scalar.activation(x[t], a_ps[t][:], ACT.Identity, bias=bias_sb[:, t : t + 1])
            nc.scalar.activation(log_neg[t][:], sig_neg[t][:], ACT.Ln, bias=floor[:])

        def softplus(t):
            nc.vector.scalar_tensor_tensor(h1[t][:], log_neg[t][:], -1.0, x[t], ALU.mult, ALU.max)

        wor_bf = sb("wor_bf", [P, PACK, P, PACK], BF16)
        wor_codes = sb("wor_codes", [P, F], U32)
        wor_scales = sb("wor_scales", [P, F], U8)

        def denominator_log(t):
            nc.scalar.activation(d_abs[t][:], d_part[t][:], ACT.Abs, bias=reserve_sb[:, t : t + 1])
            nc.scalar.activation(d_log[:, t * M : (t + 1) * M], d_abs[t][:], ACT.Ln)

        def first_factor(t):
            nc.scalar.activation(square[t][:], look_a[t][:], ACT.Square, bias=half_c[:, t : t + 1])
            nc.scalar.activation(u[t][:], square[t][:], ACT.Identity, bias=neg_quarter[:, t : t + 1], scale=rs_sb[:, t : t + 1])

        def round_wor(quarter):
            places = P // PACK
            round_and_deal(nc.scalar.copy, wor_bf[:, :, quarter * places : (quarter + 1) * places, :], wor_raw[:, :, quarter * P : (quarter + 1) * P])

        def denominator(t):
            nc.vector.scalar_tensor_tensor(d_part[t][:], look_b[t][:], 1.0, look_a[t][:], ALU.add, ALU.mult)

        def look_up_h1(t):
            nc.vector.tensor_copy(look_a[t][:], h1[t][:].indirect(first[:]))
            nc.vector.tensor_copy(look_b[t][:], h1[t][:].indirect(second[:]))

        softplus(0)
        for t in range(LAST):
            look_up_h1(t)
            softplus(t + 1)
            denominator(t)
            first_factor(t)
            denominator_log(t)
            round_wor(t)

        term_b = sb("term_b", [P, PACK, M], F32, after="x%d" % LAST)
        term_a = sb("term_a", [P, PACK, M], F32, after="log_neg%d" % LAST)

        def make_term_a(t):
            nc.vector.tensor_tensor(term_a[:, t, :], th1[t][:].indirect(first[:]), look_b[t][:], ALU.mult)

        def make_term_b(t):
            nc.vector.tensor_tensor(term_b[:, t, :], th1[t][:].indirect(second[:]), u[t][:], ALU.mult)

        def numerator(t, cols):
            nc.vector.scalar_tensor_tensor(num[:, t, cols], term_a[:, t, cols], c_rs[:, t : t + 1], term_b[:, t, cols], ALU.mult, ALU.add)

        look_up_h1(LAST)
        make_term_a(0)
        denominator(LAST)
        first_factor(LAST)
        denominator_log(LAST)
        nc.scalar.activation(inv_sq[:], d_log[:], ACT.Exp, scale=-2.0)
        round_wor(LAST)

        for t in range(PACK):
            make_term_b(t)
            if t < LAST:
                make_term_a(t + 1)
            if t > 0:
                numerator(t - 1, slice(0, M))

        y_codes = sb("y_codes", [P, M], U32)
        y_scales = sb("y_scales", [P, M], U8)
        out_rows = out_0.rearrange("(p t) m -> p t m", t=PACK)
        out_words = out_1[0].rearrange("p m t -> p (m t)").bitcast(I32)

        def by_deal(ap):
            return ap.rearrange("p t (c i) -> p c t i", i=LINE)

        def by_word(ap):
            return ap.rearrange("p (c i) t -> p c t i", i=LINE)

        fo_bf = [sb("fo_bf%d" % h, [P, HALF, PACK], BF16) for h in range(2)]
        fo_codes = [sb("fo_codes%d" % h, [P, HALF], U32) for h in range(2)]
        fo_scales = [sb("fo_scales%d" % h, [P, HALF], U8) for h in range(2)]
        y = [sb("y%d" % h, [P, PACK, HALF], F32) for h in range(2)]
        y_bf = [sb("y_bf%d" % h, [P, HALF, PACK], BF16) for h in range(2)]
        halves = [slice(h * HALF, (h + 1) * HALF) for h in range(2)]
        inv_sq_deals = inv_sq[:].rearrange("p (t m) -> p t m", t=PACK)

        def quotient(h):
            nc.vector.tensor_tensor(by_word(fo_bf[h][:]), by_deal(num[:, :, halves[h]]), by_deal(inv_sq_deals[:, :, halves[h]]), ALU.mult)

        def last_layer(h):
            nc.vector.quantize_mx(out=fo_codes[h][:].bitcast(FP8X4), scales=fo_scales[h][:], in_=fo_bf[h][:].rearrange("p m t -> p (m t)"))
            bank = psum.tile([P, PACK * HALF], F32, name="ta_ps%d" % h)
            for t in range(PACK):
                nc.tensor.matmul_mx(out=bank[:, t * HALF : (t + 1) * HALF], lhsT=wor_codes[:, deal(t)].bitcast(FP8X4), lhsT_scale=wor_scales[:, deal(t)], rhs=fo_codes[h][:].bitcast(FP8X4), rhs_scale=fo_scales[h][:], start=True, stop=True)
            return bank

        numerator(LAST, halves[0])
        numerator(LAST, halves[1])
        quotient(0)
        nc.vector.quantize_mx(out=wor_codes[:].bitcast(FP8X4), scales=wor_scales[:], in_=wor_bf[:].rearrange("p t n j -> p (t n j)"))
        yo_ps = [last_layer(0)]
        quotient(1)
        yo_ps.append(last_layer(1))
        for h in range(2):
            nc.vector.tensor_tensor(y[h][:], yo_ps[h][:].rearrange("p (t m) -> p t m", t=PACK), res_sb[:, :, halves[h]], ALU.add)
            nc.sync.dma_start(out=out_rows[:, :, halves[h]], in_=y[h][:])

        def round_y(copy, h, cols):
            copy(by_word(y_bf[h][:, cols, :]), by_deal(y[h][:, :, cols]))

        def quantize_y(h):
            nc.vector.quantize_mx(out=y_codes[:, halves[h]].bitcast(FP8X4), scales=y_scales[:, halves[h]], in_=y_bf[h][:].rearrange("p m t -> p (m t)"))
            nc.sync.dma_start(out=out_words[:, halves[h]], in_=y_codes[:, halves[h]].bitcast(I32))

        round_y(nc.scalar.copy, 0, slice(0, HALF))
        round_y(nc.scalar.copy, 1, slice(0, Y_SCALAR_COLUMNS))
        quantize_y(0)
        round_y(nc.vector.tensor_copy, 1, slice(Y_SCALAR_COLUMNS, HALF))
        quantize_y(1)
        for q, queue in enumerate((nc.scalar, nc.scalar, nc.sync, nc.sync)):
            queue.dma_start(out=out_2[0, 4 * q : 4 * q + 4, :].bitcast(I32), in_=y_scales[32 * q : 32 * q + 4, :].bitcast(I32))
